import numpy as np
import ml_dtypes


def mxq(x, axis, fmt="e4m3"):
    dtype, down = {"e4m3": (ml_dtypes.float8_e4m3fn, 7), "e5m2": (ml_dtypes.float8_e5m2, 14)}[fmt]
    v = np.moveaxis(np.asarray(x, np.float32).astype(ml_dtypes.bfloat16).astype(np.float64), axis, -1)
    blocks = v.reshape(v.shape[:-1] + (-1, 32))
    amax = np.abs(blocks).max(-1, keepdims=True)
    byte = np.maximum(np.where(amax > 0, np.frexp(amax)[1] - 1 + 127, 0) - down, 1)
    scale = np.exp2(byte - 127.0)
    codes = (blocks / scale).astype(np.float32).astype(dtype).astype(np.float64)
    return np.moveaxis((codes * scale).reshape(v.shape), -1, axis)


WIDE = False


def mx_kscale(k):
    if not WIDE:
        return np.ones(k)
    levels = np.array([10, -10, 5, -5, 0])
    if k % 512:
        return np.exp2(np.random.permutation(np.resize(levels, k // 32))).repeat(32)
    a = np.empty((k // 512, 16))
    for p in range(k // 512):
        a[p, :8] = np.random.permutation(np.resize(levels, 8))
        for g in range(8):
            far = levels[np.abs(levels - a[p, g]) >= 10]
            a[p, g + 8] = far[np.random.randint(len(far))]
    return np.exp2(a.ravel()).repeat(32)


def f64(x):
    return np.asarray(x).astype(np.float64)


def striped(idx):
    return np.tile(idx.reshape(-1, 16).T, (8, 1)).astype(np.uint16)


def unstriped(offs):
    return offs[:16].T.reshape(-1).astype(np.int64)


E2M1 = np.array([0.0, 0.5, 1.0, 1.5, 2.0, 3.0, 4.0, 6.0, -0.0, -0.5, -1.0, -1.5, -2.0, -3.0, -4.0, -6.0])


def pack_weight(w, fmt):
    k, n = w.shape
    w = f64(np.asarray(w, np.float32).astype(ml_dtypes.bfloat16)).reshape(k // 32, 32, n)
    amax = np.abs(w).max(1)
    if fmt == "e4m3":
        byte = np.frexp(amax)[1] - 1 + 127 - 7
    else:
        mant, ex = np.frexp(amax / 6.0)
        byte = np.where(mant > 0.5, ex, ex - 1) + 127
    byte = np.clip(np.where(amax > 0, byte, 1), 1, 254)
    scaled = (w * np.exp2(127.0 - byte)[:, None, :]).reshape(k, n).astype(np.float32)
    by_word = np.ascontiguousarray(scaled.reshape(k // 512, 128, 4, n).transpose(0, 1, 3, 2))
    if fmt == "e4m3":
        words = by_word.astype(ml_dtypes.float8_e4m3fn).view(np.uint8)
    else:
        c = by_word.astype(ml_dtypes.float4_e2m1fn).view(np.uint8) & 0xF
        words = (c[..., 0::2] | (c[..., 1::2] << 4)).reshape(k // 512, 128, 2 * n)
    return np.ascontiguousarray(words), np.ascontiguousarray(byte.astype(np.uint8).reshape(k // 512, 16, n))


def unpack_weight(words, scales, fmt):
    g, _, n = scales.shape
    words = np.ascontiguousarray(words).reshape(g, 128, n, -1)
    if fmt == "e4m3":
        vals = words.view(ml_dtypes.float8_e4m3fn).astype(np.float64)
    else:
        nib = np.empty((g, 128, n, 4), np.uint8)
        nib[..., 0::2] = words & 0xF
        nib[..., 1::2] = words >> 4
        vals = E2M1[nib]
    vals = vals * np.repeat(np.exp2(scales.astype(np.float64) - 127.0), 8, axis=1)[..., None]
    return vals.transpose(0, 1, 3, 2).reshape(g * 512, n)


K, T, E, C, N = 512, 1024, 8, 128, 1024


def by_expert(wq, xq):
    return np.concatenate([wq[e].T @ xq[:, e * C:(e + 1) * C] for e in range(E)], axis=1)


def setup_inputs():
    n = np.random.standard_normal
    s = mx_kscale(N)[:, None]
    w = [pack_weight(m, "e2m1") for m in n((E, N, K)) / np.sqrt(N) / s[None]]
    return {
        "dyT": (n((N, T)) * s).astype(np.float32),
        "w_words": np.stack([m[0] for m in w]),
        "w_scales": np.stack([m[1] for m in w]),
        "gate": np.tile(np.random.uniform(0.2, 1.0, E * C), (N, 1)).astype(np.float32),
        "offs": striped(np.random.permutation(T)[:E * C]),
    }


def reference(dyT, w_words, w_scales, gate, offs):
    idx = unstriped(offs)
    w = np.stack([unpack_weight(w_words[e], w_scales[e], "e2m1") for e in range(E)])
    gq = mxq(f64(gate) * f64(dyT)[:, idx], 0, "e4m3")
    dx = by_expert(w, gq)
    out = np.zeros((K, T))
    out[:, idx] = dx
    return out

@@ -1,0 +1,126 @@
+from contextlib import ExitStack
+
+import concourse.mybir as mybir
+
+F32 = mybir.dt.float32
+BF16 = mybir.dt.bfloat16
+I32 = mybir.dt.int32
+U32 = mybir.dt.uint32
+U16 = mybir.dt.uint16
+U8 = mybir.dt.uint8
+E4M3X4 = mybir.dt.float8_e4m3fn_x4
+E2M1X4 = mybir.dt.float4_e2m1fn_x4
+MULT = mybir.AluOpType.mult
+
+P = 128
+K, T, E, C, N = 512, 1024, 8, 128, 1024
+PASSES = N // 512
+KC = K // P
+HALVES = 2
+S_HALF = E * C // HALVES
+E_HALF = E // HALVES
+
+FLOPS = 2 * K * N * E * C
+BYTES = 4 * N * T + E * N * K // 2 + E * N * K // 32 + 4 * E * C + 2 * E * C + 4 * K * T
+
+
+def tile_moe_bdx_lin_none_kernel(tc, dyT, w_words, w_scales, gate, offs, out):
+    nc = tc.nc
+    with ExitStack() as ctx:
+        keep = ctx.enter_context(tc.tile_pool(name="keep", bufs=1))
+        psum = ctx.enter_context(tc.psum_pool(name="psum", bufs=1))
+
+        offsets = keep.tile([P, E * C // 16], U16, name="offsets")
+        gates = [keep.tile([P, S_HALF], F32, name=f"gate{h}") for h in range(HALVES)]
+        dy = [[keep.tile([P, T], F32, name=f"dy{a}_{t}") for t in range(4)] for a in range(PASSES)]
+        words = keep.tile([P, E * PASSES, 2 * K], U8, name="words", align_bytes=256)
+        wscale = keep.tile([P, E * PASSES, K], U8, name="wscale", align_bytes=256)
+        prod = [[keep.tile([P, 4, S_HALF], F32, name=f"prod{h}_{a}") for a in range(PASSES)] for h in range(HALVES)]
+        grouped = [[keep.tile([P, S_HALF, 4], BF16, name=f"grouped{h}_{a}", align_bytes=256) for a in range(PASSES)] for h in range(HALVES)]
+        codes = [[keep.tile([P, S_HALF], U32, name=f"codes{h}_{a}", align_bytes=256) for a in range(PASSES)] for h in range(HALVES)]
+        gscale = [[keep.tile([P, S_HALF], U8, name=f"gscale{h}_{a}", align_bytes=256) for a in range(PASSES)] for h in range(HALVES)]
+        sums = [[keep.tile([P, S_HALF], F32, name=f"sums{h}_{c}") for c in range(KC)] for h in range(HALVES)]
+        win = [keep.tile([P, T], F32, name=f"win{c}") for c in range(KC)]
+        acc = [[psum.tile([P, S_HALF], F32, name=f"acc{h}_{c}") for c in range(KC)] for h in range(HALVES)]
+
+        dyT_v = dyT.rearrange("(a p t) n -> a t p n", p=P, t=4)
+
+        nc.sync.dma_start(offsets[:], offs)
+        nc.sync.dma_start(out=gates[0][:], in_=gate[0:P, 0:S_HALF])
+        for a in range(PASSES):
+            for t in range(4):
+                nc.sync.dma_start(out=dy[a][t][:], in_=dyT_v[a, t])
+        nc.vector.memset(wscale[:].rearrange("p a k -> p (a k)").bitcast(I32), 0)
+        nc.sync.dma_start(out=gates[1][:], in_=gate[0:P, S_HALF : 2 * S_HALF])
+        for q in range(4):
+            nc.sync.dma_start(
+                out=wscale[32 * q : 32 * q + 4, :, :].bitcast(I32),
+                in_=w_scales[:, :, 4 * q : 4 * q + 4, :].rearrange("e a f k -> f (e a) k").bitcast(I32),
+            )
+        for e in range(0, E, 2):
+            nc.sync.dma_start(
+                out=words[:, PASSES * e : PASSES * (e + 2), :].bitcast(I32),
+                in_=w_words[e : e + 2].rearrange("e a p b -> p (e a) b").bitcast(I32),
+            )
+
+        cols = S_HALF // 16
+
+        def gather(h, a):
+            for t in range(4):
+                nc.vector.tensor_tensor(
+                    prod[h][a][:, t, :],
+                    dy[a][t][:].indirect(offsets[:, h * cols : (h + 1) * cols]),
+                    gates[h][:],
+                    MULT,
+                )
+
+        def interleave(h, a):
+            nc.scalar.copy(out=grouped[h][a][:], in_=prod[h][a][:].rearrange("p t s -> p s t"))
+
+        def quantise(h, a):
+            nc.vector.quantize_mx(
+                out=codes[h][a][:].bitcast(E4M3X4),
+                scales=gscale[h][a][:],
+                in_=grouped[h][a][:].rearrange("p s t -> p (s t)"),
+            )
+
+        def multiply(h):
+            for c in range(KC):
+                for i in range(E_HALF):
+                    e = h * E_HALF + i
+                    s = slice(i * C, (i + 1) * C)
+                    for a in range(PASSES):
+                        nc.tensor.matmul_mx(
+                            out=acc[h][c][:, s],
+                            lhsT=words[:, PASSES * e + a, 2 * P * c : 2 * P * (c + 1)].bitcast(E2M1X4),
+                            lhsT_scale=wscale[:, PASSES * e + a, P * c : P * (c + 1)],
+                            rhs=codes[h][a][:, s].bitcast(E4M3X4),
+                            rhs_scale=gscale[h][a][:, s],
+                            start=(a == 0),
+                            stop=(a == PASSES - 1),
+                        )
+                nc.scalar.copy(out=sums[h][c][:], in_=acc[h][c][:])
+
+        def scatter(h, c):
+            nc.vector.tensor_copy(win[c][:].indirect(offsets[:, h * cols : (h + 1) * cols]), sums[h][c][:])
+
+        gather(0, 0)
+        interleave(0, 0)
+        gather(0, 1)
+        interleave(0, 1)
+        quantise(0, 0)
+        gather(1, 0)
+        interleave(1, 0)
+        quantise(0, 1)
+        multiply(0)
+        gather(1, 1)
+        interleave(1, 1)
+        quantise(1, 0)
+        scatter(0, 0)
+        quantise(1, 1)
+        multiply(1)
+        for c in range(1, KC):
+            scatter(0, c)
+        for c in range(KC):
+            scatter(1, c)
+            nc.sync.dma_start(out=out[P * c : P * (c + 1), :], in_=win[c][:])

@@ -19,6 +19,7 @@ KC = K // P
 HALVES = 2
 S_HALF = E * C // HALVES
 E_HALF = E // HALVES
+FIRST = 128
 
 FLOPS = 2 * K * N * E * C
 BYTES = 4 * N * T + E * N * K // 2 + E * N * K // 32 + 4 * E * C + 2 * E * C + 4 * K * T
@@ -28,6 +29,7 @@ def tile_moe_bdx_lin_none_kernel(tc, dyT, w_words, w_scales, gate, offs, out):
     nc = tc.nc
     with ExitStack() as ctx:
         keep = ctx.enter_context(tc.tile_pool(name="keep", bufs=1))
+        ring = ctx.enter_context(tc.tile_pool(name="ring", bufs=2))
         psum = ctx.enter_context(tc.psum_pool(name="psum", bufs=1))
 
         offsets = keep.tile([P, E * C // 16], U16, name="offsets")
@@ -35,21 +37,25 @@ def tile_moe_bdx_lin_none_kernel(tc, dyT, w_words, w_scales, gate, offs, out):
         dy = [[keep.tile([P, T], F32, name=f"dy{a}_{t}") for t in range(4)] for a in range(PASSES)]
         words = keep.tile([P, E * PASSES, 2 * K], U8, name="words", align_bytes=256)
         wscale = keep.tile([P, E * PASSES, K], U8, name="wscale", align_bytes=256)
-        prod = [[keep.tile([P, 4, S_HALF], F32, name=f"prod{h}_{a}") for a in range(PASSES)] for h in range(HALVES)]
-        grouped = [[keep.tile([P, S_HALF, 4], BF16, name=f"grouped{h}_{a}", align_bytes=256) for a in range(PASSES)] for h in range(HALVES)]
-        codes = [[keep.tile([P, S_HALF], U32, name=f"codes{h}_{a}", align_bytes=256) for a in range(PASSES)] for h in range(HALVES)]
+        prod = [[None] * PASSES for h in range(HALVES)]
+        grouped = [[None] * PASSES for h in range(HALVES)]
+        codes = [[None] * PASSES for h in range(HALVES)]
         gscale = [[keep.tile([P, S_HALF], U8, name=f"gscale{h}_{a}", align_bytes=256) for a in range(PASSES)] for h in range(HALVES)]
-        sums = [[keep.tile([P, S_HALF], F32, name=f"sums{h}_{c}") for c in range(KC)] for h in range(HALVES)]
-        win = [keep.tile([P, T], F32, name=f"win{c}") for c in range(KC)]
+        sums_first = keep.tile([P, S_HALF], F32, name="sums_first", tag="early", align_bytes=256)
+        sums = [keep.tile([P, HALVES * S_HALF], F32, name=f"sums{c}") for c in range(KC)]
+        win = [None if c == 1 else keep.tile([P, T + 352], F32, name=f"win{c}") for c in range(KC)]
         acc = [[psum.tile([P, S_HALF], F32, name=f"acc{h}_{c}") for c in range(KC)] for h in range(HALVES)]
 
         dyT_v = dyT.rearrange("(a p t) n -> a t p n", p=P, t=4)
 
         nc.sync.dma_start(offsets[:], offs)
-        nc.sync.dma_start(out=gates[0][:], in_=gate[0:P, 0:S_HALF])
+        nc.sync.dma_start(out=gates[0][:, 0:FIRST], in_=gate[0:P, 0:FIRST])
+        nc.sync.dma_start(out=dy[0][0][:], in_=dyT_v[0, 0])
+        nc.sync.dma_start(out=gates[0][:, FIRST:S_HALF], in_=gate[0:P, FIRST:S_HALF])
         for a in range(PASSES):
             for t in range(4):
-                nc.sync.dma_start(out=dy[a][t][:], in_=dyT_v[a, t])
+                if (a, t) != (0, 0):
+                    nc.sync.dma_start(out=dy[a][t][:], in_=dyT_v[a, t])
         nc.vector.memset(wscale[:].rearrange("p a k -> p (a k)").bitcast(I32), 0)
         nc.sync.dma_start(out=gates[1][:], in_=gate[0:P, S_HALF : 2 * S_HALF])
         for q in range(4):
@@ -63,21 +69,33 @@ def tile_moe_bdx_lin_none_kernel(tc, dyT, w_words, w_scales, gate, offs, out):
                 in_=w_words[e : e + 2].rearrange("e a p b -> p (e a) b").bitcast(I32),
             )
 
-        cols = S_HALF // 16
-
         def gather(h, a):
+            prod[h][a] = (
+                keep.tile([P, 4, S_HALF], F32, name=f"prod0_{a}", align_bytes=256)
+                if h == 0
+                else ring.tile([P, 4, S_HALF], F32, name=f"prod1_{a}", tag="ring", align_bytes=256)
+            )
             for t in range(4):
-                nc.vector.tensor_tensor(
-                    prod[h][a][:, t, :],
-                    dy[a][t][:].indirect(offsets[:, h * cols : (h + 1) * cols]),
-                    gates[h][:],
-                    MULT,
-                )
+                cuts = (0, FIRST, S_HALF) if (h, a, t) == (0, 0, 0) else (0, S_HALF)
+                for lo, hi in zip(cuts[:-1], cuts[1:]):
+                    nc.vector.tensor_tensor(
+                        prod[h][a][:, t, lo:hi],
+                        dy[a][t][:].indirect(offsets[:, (h * S_HALF + lo) // 16 : (h * S_HALF + hi) // 16]),
+                        gates[h][:, lo:hi],
+                        MULT,
+                    )
 
         def interleave(h, a):
+            grouped[h][a] = (
+                ring.tile([P, S_HALF, 4], BF16, name=f"grouped0_{a}", tag="ring", align_bytes=256)
+                if h == 0
+                else keep.tile([P, S_HALF, 4], BF16, name=f"grouped1_{a}", tag="chain" if a == 1 else "grouped1_0", align_bytes=256)
+            )
             nc.scalar.copy(out=grouped[h][a][:], in_=prod[h][a][:].rearrange("p t s -> p s t"))
 
         def quantise(h, a):
+            tag = {(0, 1): "chain", (1, 1): "early"}.get((h, a), f"codes{h}_{a}")
+            codes[h][a] = keep.tile([P, S_HALF], U32, name=f"codes{h}_{a}", tag=tag, align_bytes=256)
             nc.vector.quantize_mx(
                 out=codes[h][a][:].bitcast(E4M3X4),
                 scales=gscale[h][a][:],
@@ -99,10 +117,13 @@ def tile_moe_bdx_lin_none_kernel(tc, dyT, w_words, w_scales, gate, offs, out):
                             start=(a == 0),
                             stop=(a == PASSES - 1),
                         )
-                nc.scalar.copy(out=sums[h][c][:], in_=acc[h][c][:])
 
-        def scatter(h, c):
-            nc.vector.tensor_copy(win[c][:].indirect(offsets[:, h * cols : (h + 1) * cols]), sums[h][c][:])
+        def evacuate(h, c):
+            to = sums_first[:] if (h, c) == (0, 0) else sums[c][:, h * S_HALF : (h + 1) * S_HALF]
+            nc.scalar.copy(out=to, in_=acc[h][c][:])
+
+        def scatter(c, lo, hi):
+            nc.vector.tensor_copy(win[c][:].indirect(offsets[:, lo // 16 : hi // 16]), sums_first[:] if (c, lo) == (0, 0) else sums[c][:, lo:hi])
 
         gather(0, 0)
         interleave(0, 0)
@@ -113,14 +134,18 @@ def tile_moe_bdx_lin_none_kernel(tc, dyT, w_words, w_scales, gate, offs, out):
         interleave(1, 0)
         quantise(0, 1)
         multiply(0)
+        for c in range(KC):
+            evacuate(0, c)
         gather(1, 1)
         interleave(1, 1)
         quantise(1, 0)
-        scatter(0, 0)
+        scatter(0, 0, S_HALF)
         quantise(1, 1)
         multiply(1)
-        for c in range(1, KC):
-            scatter(0, c)
+        win[1] = keep.tile([P, T + 352], F32, name="win1", tag="chain", align_bytes=256)
+        scatter(1, 0, S_HALF)
         for c in range(KC):
-            scatter(1, c)
-            nc.sync.dma_start(out=out[P * c : P * (c + 1), :], in_=win[c][:])
+            evacuate(1, c)
+        for c in range(KC):
+            scatter(c, S_HALF if c < 2 else 0, HALVES * S_HALF)
+            nc.sync.dma_start(out=out[P * c : P * (c + 1), :], in_=win[c][:, 0:T])

from contextlib import ExitStack

import concourse.mybir as mybir

F32 = mybir.dt.float32
BF16 = mybir.dt.bfloat16
I32 = mybir.dt.int32
U32 = mybir.dt.uint32
U16 = mybir.dt.uint16
U8 = mybir.dt.uint8
E4M3X4 = mybir.dt.float8_e4m3fn_x4
E2M1X4 = mybir.dt.float4_e2m1fn_x4
MULT = mybir.AluOpType.mult

P = 128
K, T, E, C, N = 512, 1024, 8, 128, 1024
PASSES = N // 512
KC = K // P
HALVES = 2
S_HALF = E * C // HALVES
E_HALF = E // HALVES
FIRST = 128

FLOPS = 2 * K * N * E * C
BYTES = 4 * N * T + E * N * K // 2 + E * N * K // 32 + 4 * E * C + 2 * E * C + 4 * K * T


def tile_moe_bdx_lin_none_kernel(tc, dyT, w_words, w_scales, gate, offs, out):
    nc = tc.nc
    with ExitStack() as ctx:
        keep = ctx.enter_context(tc.tile_pool(name="keep", bufs=1))
        ring = ctx.enter_context(tc.tile_pool(name="ring", bufs=2))
        psum = ctx.enter_context(tc.psum_pool(name="psum", bufs=1))

        offsets = keep.tile([P, E * C // 16], U16, name="offsets")
        gates = [keep.tile([P, S_HALF], F32, name=f"gate{h}") for h in range(HALVES)]
        dy = [[keep.tile([P, T], F32, name=f"dy{a}_{t}") for t in range(4)] for a in range(PASSES)]
        words = keep.tile([P, E * PASSES, 2 * K], U8, name="words", align_bytes=256)
        wscale = keep.tile([P, E * PASSES, K], U8, name="wscale", align_bytes=256)
        prod = [[None] * PASSES for h in range(HALVES)]
        grouped = [[None] * PASSES for h in range(HALVES)]
        codes = [[None] * PASSES for h in range(HALVES)]
        gscale = [[keep.tile([P, S_HALF], U8, name=f"gscale{h}_{a}", align_bytes=256) for a in range(PASSES)] for h in range(HALVES)]
        sums_first = keep.tile([P, S_HALF], F32, name="sums_first", tag="early", align_bytes=256)
        sums = [keep.tile([P, HALVES * S_HALF], F32, name=f"sums{c}") for c in range(KC)]
        win = [None if c == 1 else keep.tile([P, T + 352], F32, name=f"win{c}") for c in range(KC)]
        acc = [[psum.tile([P, S_HALF], F32, name=f"acc{h}_{c}") for c in range(KC)] for h in range(HALVES)]

        dyT_v = dyT.rearrange("(a p t) n -> a t p n", p=P, t=4)

        nc.sync.dma_start(offsets[:], offs)
        nc.sync.dma_start(out=gates[0][:, 0:FIRST], in_=gate[0:P, 0:FIRST])
        nc.sync.dma_start(out=dy[0][0][:], in_=dyT_v[0, 0])
        nc.sync.dma_start(out=gates[0][:, FIRST:S_HALF], in_=gate[0:P, FIRST:S_HALF])
        for a in range(PASSES):
            for t in range(4):
                if (a, t) != (0, 0):
                    nc.sync.dma_start(out=dy[a][t][:], in_=dyT_v[a, t])
        nc.vector.memset(wscale[:].rearrange("p a k -> p (a k)").bitcast(I32), 0)
        nc.sync.dma_start(out=gates[1][:], in_=gate[0:P, S_HALF : 2 * S_HALF])
        for q in range(4):
            nc.sync.dma_start(
                out=wscale[32 * q : 32 * q + 4, :, :].bitcast(I32),
                in_=w_scales[:, :, 4 * q : 4 * q + 4, :].rearrange("e a f k -> f (e a) k").bitcast(I32),
            )
        for e in range(0, E, 2):
            nc.sync.dma_start(
                out=words[:, PASSES * e : PASSES * (e + 2), :].bitcast(I32),
                in_=w_words[e : e + 2].rearrange("e a p b -> p (e a) b").bitcast(I32),
            )

        def gather(h, a):
            prod[h][a] = (
                keep.tile([P, 4, S_HALF], F32, name=f"prod0_{a}", align_bytes=256)
                if h == 0
                else ring.tile([P, 4, S_HALF], F32, name=f"prod1_{a}", tag="ring", align_bytes=256)
            )
            for t in range(4):
                cuts = (0, FIRST, S_HALF) if (h, a, t) == (0, 0, 0) else (0, S_HALF)
                for lo, hi in zip(cuts[:-1], cuts[1:]):
                    nc.vector.tensor_tensor(
                        prod[h][a][:, t, lo:hi],
                        dy[a][t][:].indirect(offsets[:, (h * S_HALF + lo) // 16 : (h * S_HALF + hi) // 16]),
                        gates[h][:, lo:hi],
                        MULT,
                    )

        def interleave(h, a):
            grouped[h][a] = (
                ring.tile([P, S_HALF, 4], BF16, name=f"grouped0_{a}", tag="ring", align_bytes=256)
                if h == 0
                else keep.tile([P, S_HALF, 4], BF16, name=f"grouped1_{a}", tag="chain" if a == 1 else "grouped1_0", align_bytes=256)
            )
            nc.scalar.copy(out=grouped[h][a][:], in_=prod[h][a][:].rearrange("p t s -> p s t"))

        def quantise(h, a):
            tag = {(0, 1): "chain", (1, 1): "early"}.get((h, a), f"codes{h}_{a}")
            codes[h][a] = keep.tile([P, S_HALF], U32, name=f"codes{h}_{a}", tag=tag, align_bytes=256)
            nc.vector.quantize_mx(
                out=codes[h][a][:].bitcast(E4M3X4),
                scales=gscale[h][a][:],
                in_=grouped[h][a][:].rearrange("p s t -> p (s t)"),
            )

        def multiply(h):
            for c in range(KC):
                for i in range(E_HALF):
                    e = h * E_HALF + i
                    s = slice(i * C, (i + 1) * C)
                    for a in range(PASSES):
                        nc.tensor.matmul_mx(
                            out=acc[h][c][:, s],
                            lhsT=words[:, PASSES * e + a, 2 * P * c : 2 * P * (c + 1)].bitcast(E2M1X4),
                            lhsT_scale=wscale[:, PASSES * e + a, P * c : P * (c + 1)],
                            rhs=codes[h][a][:, s].bitcast(E4M3X4),
                            rhs_scale=gscale[h][a][:, s],
                            start=(a == 0),
                            stop=(a == PASSES - 1),
                        )

        def evacuate(h, c):
            to = sums_first[:] if (h, c) == (0, 0) else sums[c][:, h * S_HALF : (h + 1) * S_HALF]
            nc.scalar.copy(out=to, in_=acc[h][c][:])

        def scatter(c, lo, hi):
            nc.vector.tensor_copy(win[c][:].indirect(offsets[:, lo // 16 : hi // 16]), sums_first[:] if (c, lo) == (0, 0) else sums[c][:, lo:hi])

        gather(0, 0)
        interleave(0, 0)
        gather(0, 1)
        interleave(0, 1)
        quantise(0, 0)
        gather(1, 0)
        interleave(1, 0)
        quantise(0, 1)
        multiply(0)
        for c in range(KC):
            evacuate(0, c)
        gather(1, 1)
        interleave(1, 1)
        quantise(1, 0)
        scatter(0, 0, S_HALF)
        quantise(1, 1)
        multiply(1)
        win[1] = keep.tile([P, T + 352], F32, name="win1", tag="chain", align_bytes=256)
        scatter(1, 0, S_HALF)
        for c in range(KC):
            evacuate(1, c)
        for c in range(KC):
            scatter(c, S_HALF if c < 2 else 0, HALVES * S_HALF)
            nc.sync.dma_start(out=out[P * c : P * (c + 1), :], in_=win[c][:, 0:T])
